import numpy as np
import ml_dtypes


def mxq(x, axis, fmt="e4m3"):
    dtype, down = {"e4m3": (ml_dtypes.float8_e4m3fn, 7), "e5m2": (ml_dtypes.float8_e5m2, 14)}[fmt]
    v = np.moveaxis(np.asarray(x, np.float32).astype(ml_dtypes.bfloat16).astype(np.float64), axis, -1)
    blocks = v.reshape(v.shape[:-1] + (-1, 32))
    amax = np.abs(blocks).max(-1, keepdims=True)
    byte = np.maximum(np.where(amax > 0, np.frexp(amax)[1] - 1 + 127, 0) - down, 1)
    scale = np.exp2(byte - 127.0)
    codes = (blocks / scale).astype(np.float32).astype(dtype).astype(np.float64)
    return np.moveaxis((codes * scale).reshape(v.shape), -1, axis)


WIDE = False


def mx_kscale(k):
    if not WIDE:
        return np.ones(k)
    levels = np.array([10, -10, 5, -5, 0])
    if k % 512:
        return np.exp2(np.random.permutation(np.resize(levels, k // 32))).repeat(32)
    a = np.empty((k // 512, 16))
    for p in range(k // 512):
        a[p, :8] = np.random.permutation(np.resize(levels, 8))
        for g in range(8):
            far = levels[np.abs(levels - a[p, g]) >= 10]
            a[p, g + 8] = far[np.random.randint(len(far))]
    return np.exp2(a.ravel()).repeat(32)


def f64(x):
    return np.asarray(x).astype(np.float64)


def striped8(idx):
    return np.asarray(idx).reshape(8, -1, 16).transpose(0, 2, 1).reshape(128, -1).astype(np.uint16)


def unstriped8(offs):
    return offs.reshape(8, 16, -1).transpose(0, 2, 1).reshape(8, -1).astype(np.int64)


def pick8(x, idx, run):
    r = np.arange(len(x))
    return x[r[:, None], idx[r % (8 * run) // run]]


E2M1 = np.array([0.0, 0.5, 1.0, 1.5, 2.0, 3.0, 4.0, 6.0, -0.0, -0.5, -1.0, -1.5, -2.0, -3.0, -4.0, -6.0])


def pack_weight(w, fmt):
    k, n = w.shape
    w = f64(np.asarray(w, np.float32).astype(ml_dtypes.bfloat16)).reshape(k // 32, 32, n)
    amax = np.abs(w).max(1)
    if fmt == "e4m3":
        byte = np.frexp(amax)[1] - 1 + 127 - 7
    else:
        mant, ex = np.frexp(amax / 6.0)
        byte = np.where(mant > 0.5, ex, ex - 1) + 127
    byte = np.clip(np.where(amax > 0, byte, 1), 1, 254)
    scaled = (w * np.exp2(127.0 - byte)[:, None, :]).reshape(k, n).astype(np.float32)
    by_word = np.ascontiguousarray(scaled.reshape(k // 512, 128, 4, n).transpose(0, 1, 3, 2))
    if fmt == "e4m3":
        words = by_word.astype(ml_dtypes.float8_e4m3fn).view(np.uint8)
    else:
        c = by_word.astype(ml_dtypes.float4_e2m1fn).view(np.uint8) & 0xF
        words = (c[..., 0::2] | (c[..., 1::2] << 4)).reshape(k // 512, 128, 2 * n)
    return np.ascontiguousarray(words), np.ascontiguousarray(byte.astype(np.uint8).reshape(k // 512, 16, n))


def unpack_weight(words, scales, fmt):
    g, _, n = scales.shape
    words = np.ascontiguousarray(words).reshape(g, 128, n, -1)
    if fmt == "e4m3":
        vals = words.view(ml_dtypes.float8_e4m3fn).astype(np.float64)
    else:
        nib = np.empty((g, 128, n, 4), np.uint8)
        nib[..., 0::2] = words & 0xF
        nib[..., 1::2] = words >> 4
        vals = E2M1[nib]
    vals = vals * np.repeat(np.exp2(scales.astype(np.float64) - 127.0), 8, axis=1)[..., None]
    return vals.transpose(0, 1, 3, 2).reshape(g * 512, n)


D, E, T, Q, I = 512, 512, 1024, 128, 256


def setup_inputs():
    n = np.random.standard_normal
    idx = np.stack([np.random.permutation(T)[:I] for _ in range(8)])
    fd = mx_kscale(D)
    fe = mx_kscale(E)
    keysp = pack_weight(n((D, T)) / fd[:, None], "e4m3")
    return {
        "query": (n((D, Q)) * 0.4 / np.sqrt(D) * fd[:, None]).astype(np.float32),
        "keys_words": keysp[0],
        "keys_scales": keysp[1],
        "gout": (n((E, Q)) * 1 / np.sqrt(E) * fe[:, None]).astype(np.float32),
        "vals": (n((E, T)) / fe[:, None]).astype(np.float32),
        "offs": striped8(idx),
    }


def reference(query, keys_words, keys_scales, gout, vals, offs):
    idx = unstriped8(offs)
    keysu = unpack_weight(keys_words, keys_scales, "e4m3")
    queryq = mxq(f64(query), 0, "e4m3")
    a = queryq.T @ keysu
    goutq = mxq(f64(gout), 0, "e4m3")
    valsq = mxq(f64(vals), 0, "e4m3")
    dw = goutq.T @ valsq
    m1 = np.max(a, axis=1, keepdims=True)
    p = np.exp(a - m1)
    pk = np.exp(pick8(a, idx, 16) - m1)
    pf = np.zeros((Q, T))
    pf[np.arange(Q)[:, None], idx[np.arange(Q) % 128 // 16]] = pk
    z = np.sum(p, axis=1, keepdims=True)
    z2 = z - np.sum(pk, axis=1, keepdims=True)
    r = p / z
    u = (p - pf) / z2
    y = (r * (dw - np.sum(r * dw, axis=1, keepdims=True)) - u * (dw - np.sum(u * dw, axis=1, keepdims=True))) * 1024.0
    return y

@@ -1,0 +1,199 @@
+from contextlib import ExitStack
+
+import concourse.mybir as mybir
+
+D, E, T, Q, SLOTS = 512, 512, 1024, 128, 256
+FLOPS = 2 * Q * T * (D + E)
+
+F32 = mybir.dt.float32
+BF16 = mybir.dt.bfloat16
+I32 = mybir.dt.int32
+U32 = mybir.dt.uint32
+U16 = mybir.dt.uint16
+U8 = mybir.dt.uint8
+FP8X4 = mybir.dt.float8_e4m3fn_x4
+ALU = mybir.AluOpType
+ACT = mybir.ActivationFunctionType
+AX = mybir.AxisListType
+
+P = 128
+PACK = 4
+BANK = 512
+CH = 256
+OUT_SCALE = 1024.0
+
+
+def interleave(copy, grouped, raw):
+    copy(
+        out=grouped.rearrange("p (c i) j -> p c j i", i=4),
+        in_=raw.rearrange("p j (c i) -> p c j i", i=4),
+    )
+
+
+def quantize(nc, codes, scales, grouped):
+    nc.vector.quantize_mx(out=codes.bitcast(FP8X4), scales=scales, in_=grouped.rearrange("p w j -> p (w j)"))
+
+
+def tile_attend_gknockout_heads_kernel(tc, query, keys_words, keys_scales, gout, vals, offs, out):
+    nc = tc.nc
+    with ExitStack() as ctx:
+        sb = ctx.enter_context(tc.tile_pool(name="sb", bufs=1))
+        ps = ctx.enter_context(tc.psum_pool(name="ps", bufs=1))
+
+        offsets = sb.tile([P, SLOTS // 16], U16, name="offsets")
+        k_scales = sb.tile([P, T], U8, name="k_scales", align_bytes=64)
+        warm = sb.tile([P, 1], F32, name="warm")
+        nc.gpsimd.memset(warm[:], 0.0)
+        warm_out = sb.tile([P, 1], F32, name="warm_out")
+        nc.scalar.activation(out=warm_out[:], in_=warm[:], func=ACT.Exp)
+        pf = sb.tile([P, T], F32, name="pf")
+        nc.gpsimd.memset(pf[:], 0.0)
+
+        q_raw = sb.tile([P, PACK, Q], F32, name="q_raw")
+        nc.sync.dma_start(out=q_raw[:], in_=query.rearrange("(p j) w -> p j w", j=PACK))
+        for quad in range(4):
+            nc.sync.dma_start(
+                out=k_scales[32 * quad : 32 * quad + 4, :].bitcast(I32),
+                in_=keys_scales[0, 4 * quad : 4 * quad + 4, :].bitcast(I32),
+            )
+        words = keys_words[0].rearrange("p n t -> p (n t)")
+        k_codes = sb.tile([P, T], U32, name="k_codes", align_bytes=64)
+        nc.sync.dma_start(out=k_codes[:].bitcast(I32), in_=words.bitcast(I32))
+        v_view = vals.rearrange("(p j) w -> p j w", j=PACK)
+        n_ch = T // CH
+        v_raw = [sb.tile([P, PACK, CH], F32, name=f"v_raw{c}") for c in range(n_ch)]
+        g_raw = sb.tile([P, PACK, Q], F32, name="g_raw")
+        nc.sync.dma_start(out=g_raw[:], in_=gout.rearrange("(p j) w -> p j w", j=PACK))
+        nc.sync.dma_start(out=v_raw[0][:], in_=v_view[:, :, 0:CH])
+        nc.sync.dma_start(offsets[:], offs)
+        for c in range(1, n_ch):
+            nc.sync.dma_start(out=v_raw[c][:], in_=v_view[:, :, c * CH : (c + 1) * CH])
+
+        q_bf = sb.tile([P, Q, PACK], BF16, name="q_bf", align_bytes=64)
+        interleave(nc.vector.tensor_copy, q_bf[:], q_raw[:])
+        q_codes = sb.tile([P, Q], U32, name="q_codes", align_bytes=64)
+        q_scales = sb.tile([P, Q], U8, name="q_scales", align_bytes=64)
+        quantize(nc, q_codes[:], q_scales[:], q_bf[:])
+        a_sb = sb.tile([P, T], F32, name="a_sb")
+        bank_max = sb.tile([P, T // BANK], F32, name="bank_max")
+        for b in range(T // BANK):
+            cols = slice(b * BANK, (b + 1) * BANK)
+            a_ps = ps.tile([P, BANK], F32, name=f"a_ps{b}")
+            nc.tensor.matmul_mx(
+                out=a_ps[:], lhsT=q_codes[:].bitcast(FP8X4), lhsT_scale=q_scales[:],
+                rhs=k_codes[:, cols].bitcast(FP8X4), rhs_scale=k_scales[:, cols], start=True, stop=True,
+            )
+            nc.vector.tensor_scalar(
+                out=a_sb[:, cols], in0=a_ps[:], scalar1=1.0, scalar2=None, op0=ALU.mult, op1=ALU.max,
+                accum_out=bank_max[:, b : b + 1],
+            )
+        neg_max = sb.tile([P, 1], F32, name="neg_max")
+        nc.vector.tensor_reduce(out=neg_max[:], in_=bank_max[:], axis=AX.X, op=ALU.max, negate=True)
+
+        v_bf = [sb.tile([P, CH, PACK], BF16, name=f"v_bf{c}", align_bytes=64) for c in range(n_ch)]
+        g_bf = sb.tile([P, Q, PACK], BF16, name="g_bf", align_bytes=64)
+        interleave(nc.scalar.copy, g_bf[:], g_raw[:])
+        interleave(nc.scalar.copy, v_bf[0][:], v_raw[0][:])
+
+        pk = sb.tile([P, SLOTS], F32, name="pk")
+        zk = sb.tile([P, 1], F32, name="zk")
+        ak = sb.tile([P, SLOTS], F32, name="ak")
+        nc.vector.tensor_copy(ak[:], a_sb[:].indirect(offsets[:]))
+        nc.scalar.activation(out=pk[:], in_=ak[:], func=ACT.Exp, bias=neg_max[:], accum_out=zk[:])
+        p = sb.tile([P, T], F32, name="p")
+        z = sb.tile([P, 1], F32, name="z")
+        nc.scalar.activation(out=p[:], in_=a_sb[:], func=ACT.Exp, bias=neg_max[:], accum_out=z[:])
+
+        g_codes = sb.tile([P, Q], U32, name="g_codes", align_bytes=64)
+        g_scales = sb.tile([P, Q], U8, name="g_scales", align_bytes=64)
+        v_codes = [sb.tile([P, CH], U32, name=f"v_codes{c}", align_bytes=64) for c in range(n_ch)]
+        v_scales = [sb.tile([P, CH], U8, name=f"v_scales{c}", align_bytes=64) for c in range(n_ch)]
+        quantize(nc, g_codes[:], g_scales[:], g_bf[:])
+        quantize(nc, v_codes[0][:], v_scales[0][:], v_bf[0][:])
+        dw_a = ps.tile([P, 2 * CH], F32, name="dw_a")
+        dw_b = ps.tile([P, CH], F32, name="dw_b")
+        dw_c = ps.tile([P, CH], F32, name="dw_c")
+        dw = [dw_a[:, 0:CH], dw_a[:, CH : 2 * CH], dw_b[:], dw_c[:]]
+
+        def product(c):
+            nc.tensor.matmul_mx(
+                out=dw[c], lhsT=g_codes[:].bitcast(FP8X4), lhsT_scale=g_scales[:],
+                rhs=v_codes[c][:].bitcast(FP8X4), rhs_scale=v_scales[c][:], start=True, stop=True,
+            )
+
+        product(0)
+
+        nc.vector.tensor_copy(pf[:].indirect(offsets[:]), pk[:])
+
+        rz = sb.tile([P, 2], F32, name="rz")
+        z2 = sb.tile([P, 1], F32, name="z2")
+        share = sb.tile([P, 1], F32, name="share")
+        cz = sb.tile([P, 2], F32, name="cz")
+        parts = sb.tile([P, 7], F32, name="parts")
+        raw_part = sb.tile([P, 1], F32, name="raw_part")
+        junk = sb.tile([P, 2 * CH], F32, name="junk")
+        nc.vector.reciprocal(out=rz[:, 0:1], in_=z[:])
+        nc.vector.tensor_tensor(out=z2[:], in0=z[:], in1=zk[:], op=ALU.subtract)
+        nc.vector.scalar_tensor_tensor(
+            out=junk[:, 0:CH], in0=dw[0], scalar=OUT_SCALE, in1=p[:, 0:CH], op0=ALU.mult, op1=ALU.mult, accum_out=raw_part[:]
+        )
+        nc.vector.tensor_tensor(out=share[:], in0=zk[:], in1=rz[:, 0:1], op=ALU.mult)
+        nc.vector.reciprocal(out=rz[:, 1:2], in_=z2[:])
+        wn = sb.tile([P, T], F32, name="wn")
+        nc.vector.scalar_tensor_tensor(out=wn[:], in0=p[:], scalar=share[:], in1=pf[:], op0=ALU.mult, op1=ALU.subtract)
+        nc.vector.tensor_scalar(out=cz[:], in0=rz[:], scalar1=OUT_SCALE, scalar2=None, op0=ALU.mult)
+        nc.vector.tensor_tensor(out=parts[:, 3:4], in0=raw_part[:], in1=rz[:, 0:1], op=ALU.mult)
+
+        for c in range(1, n_ch):
+            interleave(nc.scalar.copy, v_bf[c][:], v_raw[c][:])
+            quantize(nc, v_codes[c][:], v_scales[c][:], v_bf[c][:])
+            product(c)
+
+        tn = sb.tile([P, T], F32, name="tn")
+        spent = v_bf[3][:].rearrange("p w j -> p (w j)").bitcast(F32)
+
+        def with_weights(src, cols, s):
+            nc.vector.scalar_tensor_tensor(
+                out=tn[:, cols], in0=src, scalar=cz[:, 1:2], in1=wn[:, cols], op0=ALU.mult, op1=ALU.mult,
+                accum_out=parts[:, s : s + 1],
+            )
+
+        def with_softmax(c, dst):
+            nc.vector.scalar_tensor_tensor(
+                out=dst, in0=dw[c], scalar=cz[:, 0:1], in1=p[:, c * CH : (c + 1) * CH], op0=ALU.mult, op1=ALU.mult,
+                accum_out=parts[:, 3 + c : 4 + c],
+            )
+
+        with_weights(dw_a[:], slice(0, 2 * CH), 0)
+        with_weights(dw_b[:], slice(2 * CH, 3 * CH), 1)
+        with_softmax(1, spent[:, 0:CH])
+        with_softmax(2, spent[:, CH : 2 * CH])
+        with_weights(dw_c[:], slice(3 * CH, 4 * CH), 2)
+        with_softmax(3, junk[:, CH : 2 * CH])
+
+        gamma = sb.tile([P, 1], F32, name="gamma")
+        k2 = sb.tile([P, 1], F32, name="k2")
+        scratch_g = sb.tile([P, 3], F32, name="scratch_g")
+        scratch_k = sb.tile([P, 7], F32, name="scratch_k")
+        nc.vector.tensor_scalar(
+            out=scratch_g[:], in0=parts[:, 0:3], scalar1=rz[:, 0:1], scalar2=None, op0=ALU.mult, op1=ALU.add, accum_out=gamma[:]
+        )
+        nc.vector.tensor_scalar(
+            out=scratch_k[:], in0=parts[:], scalar1=rz[:, 1:2], scalar2=None,
+            op0=ALU.mult, op1=ALU.add, accum_out=k2[:],
+        )
+        v = [sb.tile([P, CH], F32, name=f"v{c}") for c in range(n_ch)]
+        y = [sb.tile([P, CH], F32, name=f"y{c}") for c in range(n_ch)]
+        for step in range(n_ch + 1):
+            if step < n_ch:
+                cols = slice(step * CH, (step + 1) * CH)
+                nc.vector.scalar_tensor_tensor(
+                    out=v[step][:], in0=p[:, cols], scalar=gamma[:], in1=tn[:, cols], op0=ALU.mult, op1=ALU.subtract
+                )
+            if step > 0:
+                c = step - 1
+                cols = slice(c * CH, (c + 1) * CH)
+                nc.vector.scalar_tensor_tensor(
+                    out=y[c][:], in0=wn[:, cols], scalar=k2[:], in1=v[c][:], op0=ALU.mult, op1=ALU.add
+                )
+                nc.sync.dma_start(out=out[:, cols], in_=y[c][:])

@@ -21,6 +21,7 @@ PACK = 4
 BANK = 512
 CH = 256
 OUT_SCALE = 1024.0
+TINY = 1e-30
 
 
 def interleave(copy, grouped, raw):
@@ -46,28 +47,31 @@ def tile_attend_gknockout_heads_kernel(tc, query, keys_words, keys_scales, gout,
         nc.gpsimd.memset(warm[:], 0.0)
         warm_out = sb.tile([P, 1], F32, name="warm_out")
         nc.scalar.activation(out=warm_out[:], in_=warm[:], func=ACT.Exp)
-        pf = sb.tile([P, T], F32, name="pf")
-        nc.gpsimd.memset(pf[:], 0.0)
 
-        q_raw = sb.tile([P, PACK, Q], F32, name="q_raw")
+        q_raw = sb.tile([P, PACK, Q], F32, name="q_raw", align_bytes=256)
         nc.sync.dma_start(out=q_raw[:], in_=query.rearrange("(p j) w -> p j w", j=PACK))
         for quad in range(4):
             nc.sync.dma_start(
                 out=k_scales[32 * quad : 32 * quad + 4, :].bitcast(I32),
                 in_=keys_scales[0, 4 * quad : 4 * quad + 4, :].bitcast(I32),
             )
+        pf = sb.tile([P, T], F32, name="pf")
+        nc.gpsimd.memset(pf[:], 0.0)
+        g_raw = sb.tile([P, PACK, Q], F32, name="g_raw", align_bytes=256)
         words = keys_words[0].rearrange("p n t -> p (n t)")
-        k_codes = sb.tile([P, T], U32, name="k_codes", align_bytes=64)
-        nc.sync.dma_start(out=k_codes[:].bitcast(I32), in_=words.bitcast(I32))
+        k_codes = []
+        for b in range(T // BANK):
+            kc = sb.tile([P, BANK], U32, name=f"k_codes{b}", align_bytes=256)
+            nc.sync.dma_start(out=kc[:].bitcast(I32), in_=words[:, PACK * BANK * b : PACK * BANK * (b + 1)].bitcast(I32))
+            k_codes.append(kc)
         v_view = vals.rearrange("(p j) w -> p j w", j=PACK)
         n_ch = T // CH
-        v_raw = [sb.tile([P, PACK, CH], F32, name=f"v_raw{c}") for c in range(n_ch)]
-        g_raw = sb.tile([P, PACK, Q], F32, name="g_raw")
-        nc.sync.dma_start(out=g_raw[:], in_=gout.rearrange("(p j) w -> p j w", j=PACK))
-        nc.sync.dma_start(out=v_raw[0][:], in_=v_view[:, :, 0:CH])
-        nc.sync.dma_start(offsets[:], offs)
-        for c in range(1, n_ch):
+        v_raw = [sb.tile([P, PACK, CH], F32, name=f"v_raw{c}", tag=f"v_raw{c}", align_bytes=256) for c in range(n_ch)]
+        for c in range(n_ch):
             nc.sync.dma_start(out=v_raw[c][:], in_=v_view[:, :, c * CH : (c + 1) * CH])
+            if c == 0:
+                nc.sync.dma_start(offsets[:], offs)
+                nc.sync.dma_start(out=g_raw[:], in_=gout.rearrange("(p j) w -> p j w", j=PACK))
 
         q_bf = sb.tile([P, Q, PACK], BF16, name="q_bf", align_bytes=64)
         interleave(nc.vector.tensor_copy, q_bf[:], q_raw[:])
@@ -81,7 +85,7 @@ def tile_attend_gknockout_heads_kernel(tc, query, keys_words, keys_scales, gout,
             a_ps = ps.tile([P, BANK], F32, name=f"a_ps{b}")
             nc.tensor.matmul_mx(
                 out=a_ps[:], lhsT=q_codes[:].bitcast(FP8X4), lhsT_scale=q_scales[:],
-                rhs=k_codes[:, cols].bitcast(FP8X4), rhs_scale=k_scales[:, cols], start=True, stop=True,
+                rhs=k_codes[b][:].bitcast(FP8X4), rhs_scale=k_scales[:, cols], start=True, stop=True,
             )
             nc.vector.tensor_scalar(
                 out=a_sb[:, cols], in0=a_ps[:], scalar1=1.0, scalar2=None, op0=ALU.mult, op1=ALU.max,
@@ -91,29 +95,25 @@ def tile_attend_gknockout_heads_kernel(tc, query, keys_words, keys_scales, gout,
         nc.vector.tensor_reduce(out=neg_max[:], in_=bank_max[:], axis=AX.X, op=ALU.max, negate=True)
 
         v_bf = [sb.tile([P, CH, PACK], BF16, name=f"v_bf{c}", align_bytes=64) for c in range(n_ch)]
-        g_bf = sb.tile([P, Q, PACK], BF16, name="g_bf", align_bytes=64)
-        interleave(nc.scalar.copy, g_bf[:], g_raw[:])
         interleave(nc.scalar.copy, v_bf[0][:], v_raw[0][:])
 
+        ak = sb.tile([P, SLOTS], F32, name="ak", tag="ak_then_p")
         pk = sb.tile([P, SLOTS], F32, name="pk")
         zk = sb.tile([P, 1], F32, name="zk")
-        ak = sb.tile([P, SLOTS], F32, name="ak")
         nc.vector.tensor_copy(ak[:], a_sb[:].indirect(offsets[:]))
         nc.scalar.activation(out=pk[:], in_=ak[:], func=ACT.Exp, bias=neg_max[:], accum_out=zk[:])
-        p = sb.tile([P, T], F32, name="p")
+        p = sb.tile([P, T], F32, name="p", tag="ak_then_p")
         z = sb.tile([P, 1], F32, name="z")
         nc.scalar.activation(out=p[:], in_=a_sb[:], func=ACT.Exp, bias=neg_max[:], accum_out=z[:])
 
+        g_bf = sb.tile([P, Q, PACK], BF16, name="g_bf", align_bytes=64)
+        interleave(nc.vector.tensor_copy, g_bf[:], g_raw[:])
         g_codes = sb.tile([P, Q], U32, name="g_codes", align_bytes=64)
         g_scales = sb.tile([P, Q], U8, name="g_scales", align_bytes=64)
-        v_codes = [sb.tile([P, CH], U32, name=f"v_codes{c}", align_bytes=64) for c in range(n_ch)]
         v_scales = [sb.tile([P, CH], U8, name=f"v_scales{c}", align_bytes=64) for c in range(n_ch)]
         quantize(nc, g_codes[:], g_scales[:], g_bf[:])
-        quantize(nc, v_codes[0][:], v_scales[0][:], v_bf[0][:])
-        dw_a = ps.tile([P, 2 * CH], F32, name="dw_a")
-        dw_b = ps.tile([P, CH], F32, name="dw_b")
-        dw_c = ps.tile([P, CH], F32, name="dw_c")
-        dw = [dw_a[:, 0:CH], dw_a[:, CH : 2 * CH], dw_b[:], dw_c[:]]
+        dw_bank = [ps.tile([P, BANK], F32, name=f"dw{b}") for b in range(T // BANK)]
+        dw = [dw_bank[c // 2][:, (c % 2) * CH : (c % 2 + 1) * CH] for c in range(n_ch)]
 
         def product(c):
             nc.tensor.matmul_mx(
@@ -121,79 +121,75 @@ def tile_attend_gknockout_heads_kernel(tc, query, keys_words, keys_scales, gout,
                 rhs=v_codes[c][:].bitcast(FP8X4), rhs_scale=v_scales[c][:], start=True, stop=True,
             )
 
-        product(0)
-
+        v_codes = [sb.tile([P, CH], U32, name=f"v_codes{c}", align_bytes=64) for c in range(n_ch)]
+        half = CH // 2
         nc.vector.tensor_copy(pf[:].indirect(offsets[:]), pk[:])
+        quantize(nc, v_codes[0][:], v_scales[0][:], v_bf[0][:])
+        product(0)
+        interleave(nc.vector.tensor_copy, v_bf[2][:, half:CH, :], v_raw[2][:, :, half:CH])
 
-        rz = sb.tile([P, 2], F32, name="rz")
-        z2 = sb.tile([P, 1], F32, name="z2")
-        share = sb.tile([P, 1], F32, name="share")
-        cz = sb.tile([P, 2], F32, name="cz")
-        parts = sb.tile([P, 7], F32, name="parts")
-        raw_part = sb.tile([P, 1], F32, name="raw_part")
-        junk = sb.tile([P, 2 * CH], F32, name="junk")
-        nc.vector.reciprocal(out=rz[:, 0:1], in_=z[:])
-        nc.vector.tensor_tensor(out=z2[:], in0=z[:], in1=zk[:], op=ALU.subtract)
-        nc.vector.scalar_tensor_tensor(
-            out=junk[:, 0:CH], in0=dw[0], scalar=OUT_SCALE, in1=p[:, 0:CH], op0=ALU.mult, op1=ALU.mult, accum_out=raw_part[:]
-        )
-        nc.vector.tensor_tensor(out=share[:], in0=zk[:], in1=rz[:, 0:1], op=ALU.mult)
-        nc.vector.reciprocal(out=rz[:, 1:2], in_=z2[:])
-        wn = sb.tile([P, T], F32, name="wn")
-        nc.vector.scalar_tensor_tensor(out=wn[:], in0=p[:], scalar=share[:], in1=pf[:], op0=ALU.mult, op1=ALU.subtract)
-        nc.vector.tensor_scalar(out=cz[:], in0=rz[:], scalar1=OUT_SCALE, scalar2=None, op0=ALU.mult)
-        nc.vector.tensor_tensor(out=parts[:, 3:4], in0=raw_part[:], in1=rz[:, 0:1], op=ALU.mult)
-
-        for c in range(1, n_ch):
-            interleave(nc.scalar.copy, v_bf[c][:], v_raw[c][:])
+        def values_chunk(c):
+            width = half if c == 2 else CH
+            interleave(nc.scalar.copy, v_bf[c][:, 0:width, :], v_raw[c][:, :, 0:width])
             quantize(nc, v_codes[c][:], v_scales[c][:], v_bf[c][:])
             product(c)
 
-        tn = sb.tile([P, T], F32, name="tn")
+        rz = sb.tile([P, 1], F32, name="rz")
+        share = sb.tile([P, 1], F32, name="share")
+        den = sb.tile([P, 2], F32, name="den")
+        inv = sb.tile([P, 2], F32, name="inv")
+        nc.vector.reciprocal(out=rz[:], in_=z[:])
+        nc.vector.tensor_scalar(
+            out=den[:, 0:1], in0=z[:], scalar1=zk[:], scalar2=1.0 / OUT_SCALE, op0=ALU.subtract, op1=ALU.mult
+        )
+        nc.vector.tensor_tensor(out=share[:], in0=zk[:], in1=rz[:], op=ALU.mult)
+        wn = sb.tile([P, T], F32, name="wn")
+        nc.vector.scalar_tensor_tensor(out=wn[:], in0=p[:], scalar=share[:], in1=pf[:], op0=ALU.mult, op1=ALU.subtract)
+        nc.vector.tensor_scalar(
+            out=den[:, 1:2], in0=share[:], scalar1=TINY, scalar2=den[:, 0:1], op0=ALU.max, op1=ALU.mult
+        )
+        nc.vector.reciprocal(out=inv[:], in_=den[:])
+        for c in range(1, n_ch):
+            values_chunk(c)
+        s_parts = sb.tile([P, 2], F32, name="s_parts")
+        junk = sb.tile([P, BANK], F32, name="junk")
         spent = v_bf[3][:].rearrange("p w j -> p (w j)").bitcast(F32)
-
-        def with_weights(src, cols, s):
+        for b, dst in enumerate([spent, junk[:]]):
             nc.vector.scalar_tensor_tensor(
-                out=tn[:, cols], in0=src, scalar=cz[:, 1:2], in1=wn[:, cols], op0=ALU.mult, op1=ALU.mult,
-                accum_out=parts[:, s : s + 1],
+                out=dst, in0=dw_bank[b][:], scalar=1.0, in1=p[:, b * BANK : (b + 1) * BANK], op0=ALU.mult, op1=ALU.mult,
+                accum_out=s_parts[:, b : b + 1],
             )
 
-        def with_softmax(c, dst):
+        wc_u = sb.tile([P, 2 * T], F32, name="wc_u", tag=f"v_raw{n_ch - 1}", align_bytes=256)
+        wc = wc_u[:, 0:T]
+        u = wc_u[:, T : 2 * T]
+        for b in range(T // BANK):
+            cols = slice(b * BANK, (b + 1) * BANK)
+            nc.scalar.activation(out=wc[:, cols], in_=wn[:, cols], func=ACT.Copy, scale=inv[:, 0:1])
+        for b in range(T // BANK):
+            cols = slice(b * BANK, (b + 1) * BANK)
+            nc.scalar.activation(out=u[:, cols], in_=wn[:, cols], func=ACT.Relu, scale=inv[:, 1:2])
+
+        s1 = sb.tile([P, 1], F32, name="s1")
+        nc.vector.tensor_scalar(
+            out=s1[:], in0=s_parts[:, 0:1], scalar1=s_parts[:, 1:2], scalar2=rz[:], op0=ALU.add, op1=ALU.mult
+        )
+        t = sb.tile([P, T], F32, name="t")
+        t_parts = sb.tile([P, 2], F32, name="t_parts")
+        for b in range(T // BANK):
+            cols = slice(b * BANK, (b + 1) * BANK)
             nc.vector.scalar_tensor_tensor(
-                out=dst, in0=dw[c], scalar=cz[:, 0:1], in1=p[:, c * CH : (c + 1) * CH], op0=ALU.mult, op1=ALU.mult,
-                accum_out=parts[:, 3 + c : 4 + c],
+                out=t[:, cols], in0=dw_bank[b][:], scalar=s1[:], in1=wc[:, cols], op0=ALU.subtract, op1=ALU.mult,
+                accum_out=t_parts[:, b : b + 1],
             )
-
-        with_weights(dw_a[:], slice(0, 2 * CH), 0)
-        with_weights(dw_b[:], slice(2 * CH, 3 * CH), 1)
-        with_softmax(1, spent[:, 0:CH])
-        with_softmax(2, spent[:, CH : 2 * CH])
-        with_weights(dw_c[:], slice(3 * CH, 4 * CH), 2)
-        with_softmax(3, junk[:, CH : 2 * CH])
-
-        gamma = sb.tile([P, 1], F32, name="gamma")
-        k2 = sb.tile([P, 1], F32, name="k2")
-        scratch_g = sb.tile([P, 3], F32, name="scratch_g")
-        scratch_k = sb.tile([P, 7], F32, name="scratch_k")
+        t_sum = sb.tile([P, 1], F32, name="t_sum")
         nc.vector.tensor_scalar(
-            out=scratch_g[:], in0=parts[:, 0:3], scalar1=rz[:, 0:1], scalar2=None, op0=ALU.mult, op1=ALU.add, accum_out=gamma[:]
+            out=t_sum[:], in0=t_parts[:, 0:1], scalar1=t_parts[:, 1:2], scalar2=1.0 / OUT_SCALE, op0=ALU.add, op1=ALU.mult
         )
-        nc.vector.tensor_scalar(
-            out=scratch_k[:], in0=parts[:], scalar1=rz[:, 1:2], scalar2=None,
-            op0=ALU.mult, op1=ALU.add, accum_out=k2[:],
-        )
-        v = [sb.tile([P, CH], F32, name=f"v{c}") for c in range(n_ch)]
-        y = [sb.tile([P, CH], F32, name=f"y{c}") for c in range(n_ch)]
-        for step in range(n_ch + 1):
-            if step < n_ch:
-                cols = slice(step * CH, (step + 1) * CH)
-                nc.vector.scalar_tensor_tensor(
-                    out=v[step][:], in0=p[:, cols], scalar=gamma[:], in1=tn[:, cols], op0=ALU.mult, op1=ALU.subtract
-                )
-            if step > 0:
-                c = step - 1
-                cols = slice(c * CH, (c + 1) * CH)
-                nc.vector.scalar_tensor_tensor(
-                    out=y[c][:], in0=wn[:, cols], scalar=k2[:], in1=v[c][:], op0=ALU.mult, op1=ALU.add
-                )
-                nc.sync.dma_start(out=out[:, cols], in_=y[c][:])
+        for c in range(n_ch):
+            cols = slice(c * CH, (c + 1) * CH)
+            y = sb.tile([P, CH], F32, name=f"y{c}", align_bytes=256)
+            nc.vector.scalar_tensor_tensor(
+                out=y[:], in0=u[:, cols], scalar=t_sum[:], in1=t[:, cols], op0=ALU.mult, op1=ALU.subtract
+            )
+            nc.sync.dma_start(out=out[:, cols], in_=y[:])

from contextlib import ExitStack

import concourse.mybir as mybir

D, E, T, Q, SLOTS = 512, 512, 1024, 128, 256
FLOPS = 2 * Q * T * (D + E)

F32 = mybir.dt.float32
BF16 = mybir.dt.bfloat16
I32 = mybir.dt.int32
U32 = mybir.dt.uint32
U16 = mybir.dt.uint16
U8 = mybir.dt.uint8
FP8X4 = mybir.dt.float8_e4m3fn_x4
ALU = mybir.AluOpType
ACT = mybir.ActivationFunctionType
AX = mybir.AxisListType

P = 128
PACK = 4
BANK = 512
CH = 256
OUT_SCALE = 1024.0
TINY = 1e-30


def interleave(copy, grouped, raw):
    copy(
        out=grouped.rearrange("p (c i) j -> p c j i", i=4),
        in_=raw.rearrange("p j (c i) -> p c j i", i=4),
    )


def quantize(nc, codes, scales, grouped):
    nc.vector.quantize_mx(out=codes.bitcast(FP8X4), scales=scales, in_=grouped.rearrange("p w j -> p (w j)"))


def tile_attend_gknockout_heads_kernel(tc, query, keys_words, keys_scales, gout, vals, offs, out):
    nc = tc.nc
    with ExitStack() as ctx:
        sb = ctx.enter_context(tc.tile_pool(name="sb", bufs=1))
        ps = ctx.enter_context(tc.psum_pool(name="ps", bufs=1))

        offsets = sb.tile([P, SLOTS // 16], U16, name="offsets")
        k_scales = sb.tile([P, T], U8, name="k_scales", align_bytes=64)
        warm = sb.tile([P, 1], F32, name="warm")
        nc.gpsimd.memset(warm[:], 0.0)
        warm_out = sb.tile([P, 1], F32, name="warm_out")
        nc.scalar.activation(out=warm_out[:], in_=warm[:], func=ACT.Exp)

        q_raw = sb.tile([P, PACK, Q], F32, name="q_raw", align_bytes=256)
        nc.sync.dma_start(out=q_raw[:], in_=query.rearrange("(p j) w -> p j w", j=PACK))
        for quad in range(4):
            nc.sync.dma_start(
                out=k_scales[32 * quad : 32 * quad + 4, :].bitcast(I32),
                in_=keys_scales[0, 4 * quad : 4 * quad + 4, :].bitcast(I32),
            )
        pf = sb.tile([P, T], F32, name="pf")
        nc.gpsimd.memset(pf[:], 0.0)
        g_raw = sb.tile([P, PACK, Q], F32, name="g_raw", align_bytes=256)
        words = keys_words[0].rearrange("p n t -> p (n t)")
        k_codes = []
        for b in range(T // BANK):
            kc = sb.tile([P, BANK], U32, name=f"k_codes{b}", align_bytes=256)
            nc.sync.dma_start(out=kc[:].bitcast(I32), in_=words[:, PACK * BANK * b : PACK * BANK * (b + 1)].bitcast(I32))
            k_codes.append(kc)
        v_view = vals.rearrange("(p j) w -> p j w", j=PACK)
        n_ch = T // CH
        v_raw = [sb.tile([P, PACK, CH], F32, name=f"v_raw{c}", tag=f"v_raw{c}", align_bytes=256) for c in range(n_ch)]
        for c in range(n_ch):
            nc.sync.dma_start(out=v_raw[c][:], in_=v_view[:, :, c * CH : (c + 1) * CH])
            if c == 0:
                nc.sync.dma_start(offsets[:], offs)
                nc.sync.dma_start(out=g_raw[:], in_=gout.rearrange("(p j) w -> p j w", j=PACK))

        q_bf = sb.tile([P, Q, PACK], BF16, name="q_bf", align_bytes=64)
        interleave(nc.vector.tensor_copy, q_bf[:], q_raw[:])
        q_codes = sb.tile([P, Q], U32, name="q_codes", align_bytes=64)
        q_scales = sb.tile([P, Q], U8, name="q_scales", align_bytes=64)
        quantize(nc, q_codes[:], q_scales[:], q_bf[:])
        a_sb = sb.tile([P, T], F32, name="a_sb")
        bank_max = sb.tile([P, T // BANK], F32, name="bank_max")
        for b in range(T // BANK):
            cols = slice(b * BANK, (b + 1) * BANK)
            a_ps = ps.tile([P, BANK], F32, name=f"a_ps{b}")
            nc.tensor.matmul_mx(
                out=a_ps[:], lhsT=q_codes[:].bitcast(FP8X4), lhsT_scale=q_scales[:],
                rhs=k_codes[b][:].bitcast(FP8X4), rhs_scale=k_scales[:, cols], start=True, stop=True,
            )
            nc.vector.tensor_scalar(
                out=a_sb[:, cols], in0=a_ps[:], scalar1=1.0, scalar2=None, op0=ALU.mult, op1=ALU.max,
                accum_out=bank_max[:, b : b + 1],
            )
        neg_max = sb.tile([P, 1], F32, name="neg_max")
        nc.vector.tensor_reduce(out=neg_max[:], in_=bank_max[:], axis=AX.X, op=ALU.max, negate=True)

        v_bf = [sb.tile([P, CH, PACK], BF16, name=f"v_bf{c}", align_bytes=64) for c in range(n_ch)]
        interleave(nc.scalar.copy, v_bf[0][:], v_raw[0][:])

        ak = sb.tile([P, SLOTS], F32, name="ak", tag="ak_then_p")
        pk = sb.tile([P, SLOTS], F32, name="pk")
        zk = sb.tile([P, 1], F32, name="zk")
        nc.vector.tensor_copy(ak[:], a_sb[:].indirect(offsets[:]))
        nc.scalar.activation(out=pk[:], in_=ak[:], func=ACT.Exp, bias=neg_max[:], accum_out=zk[:])
        p = sb.tile([P, T], F32, name="p", tag="ak_then_p")
        z = sb.tile([P, 1], F32, name="z")
        nc.scalar.activation(out=p[:], in_=a_sb[:], func=ACT.Exp, bias=neg_max[:], accum_out=z[:])

        g_bf = sb.tile([P, Q, PACK], BF16, name="g_bf", align_bytes=64)
        interleave(nc.vector.tensor_copy, g_bf[:], g_raw[:])
        g_codes = sb.tile([P, Q], U32, name="g_codes", align_bytes=64)
        g_scales = sb.tile([P, Q], U8, name="g_scales", align_bytes=64)
        v_scales = [sb.tile([P, CH], U8, name=f"v_scales{c}", align_bytes=64) for c in range(n_ch)]
        quantize(nc, g_codes[:], g_scales[:], g_bf[:])
        dw_bank = [ps.tile([P, BANK], F32, name=f"dw{b}") for b in range(T // BANK)]
        dw = [dw_bank[c // 2][:, (c % 2) * CH : (c % 2 + 1) * CH] for c in range(n_ch)]

        def product(c):
            nc.tensor.matmul_mx(
                out=dw[c], lhsT=g_codes[:].bitcast(FP8X4), lhsT_scale=g_scales[:],
                rhs=v_codes[c][:].bitcast(FP8X4), rhs_scale=v_scales[c][:], start=True, stop=True,
            )

        v_codes = [sb.tile([P, CH], U32, name=f"v_codes{c}", align_bytes=64) for c in range(n_ch)]
        half = CH // 2
        nc.vector.tensor_copy(pf[:].indirect(offsets[:]), pk[:])
        quantize(nc, v_codes[0][:], v_scales[0][:], v_bf[0][:])
        product(0)
        interleave(nc.vector.tensor_copy, v_bf[2][:, half:CH, :], v_raw[2][:, :, half:CH])

        def values_chunk(c):
            width = half if c == 2 else CH
            interleave(nc.scalar.copy, v_bf[c][:, 0:width, :], v_raw[c][:, :, 0:width])
            quantize(nc, v_codes[c][:], v_scales[c][:], v_bf[c][:])
            product(c)

        rz = sb.tile([P, 1], F32, name="rz")
        share = sb.tile([P, 1], F32, name="share")
        den = sb.tile([P, 2], F32, name="den")
        inv = sb.tile([P, 2], F32, name="inv")
        nc.vector.reciprocal(out=rz[:], in_=z[:])
        nc.vector.tensor_scalar(
            out=den[:, 0:1], in0=z[:], scalar1=zk[:], scalar2=1.0 / OUT_SCALE, op0=ALU.subtract, op1=ALU.mult
        )
        nc.vector.tensor_tensor(out=share[:], in0=zk[:], in1=rz[:], op=ALU.mult)
        wn = sb.tile([P, T], F32, name="wn")
        nc.vector.scalar_tensor_tensor(out=wn[:], in0=p[:], scalar=share[:], in1=pf[:], op0=ALU.mult, op1=ALU.subtract)
        nc.vector.tensor_scalar(
            out=den[:, 1:2], in0=share[:], scalar1=TINY, scalar2=den[:, 0:1], op0=ALU.max, op1=ALU.mult
        )
        nc.vector.reciprocal(out=inv[:], in_=den[:])
        for c in range(1, n_ch):
            values_chunk(c)
        s_parts = sb.tile([P, 2], F32, name="s_parts")
        junk = sb.tile([P, BANK], F32, name="junk")
        spent = v_bf[3][:].rearrange("p w j -> p (w j)").bitcast(F32)
        for b, dst in enumerate([spent, junk[:]]):
            nc.vector.scalar_tensor_tensor(
                out=dst, in0=dw_bank[b][:], scalar=1.0, in1=p[:, b * BANK : (b + 1) * BANK], op0=ALU.mult, op1=ALU.mult,
                accum_out=s_parts[:, b : b + 1],
            )

        wc_u = sb.tile([P, 2 * T], F32, name="wc_u", tag=f"v_raw{n_ch - 1}", align_bytes=256)
        wc = wc_u[:, 0:T]
        u = wc_u[:, T : 2 * T]
        for b in range(T // BANK):
            cols = slice(b * BANK, (b + 1) * BANK)
            nc.scalar.activation(out=wc[:, cols], in_=wn[:, cols], func=ACT.Copy, scale=inv[:, 0:1])
        for b in range(T // BANK):
            cols = slice(b * BANK, (b + 1) * BANK)
            nc.scalar.activation(out=u[:, cols], in_=wn[:, cols], func=ACT.Relu, scale=inv[:, 1:2])

        s1 = sb.tile([P, 1], F32, name="s1")
        nc.vector.tensor_scalar(
            out=s1[:], in0=s_parts[:, 0:1], scalar1=s_parts[:, 1:2], scalar2=rz[:], op0=ALU.add, op1=ALU.mult
        )
        t = sb.tile([P, T], F32, name="t")
        t_parts = sb.tile([P, 2], F32, name="t_parts")
        for b in range(T // BANK):
            cols = slice(b * BANK, (b + 1) * BANK)
            nc.vector.scalar_tensor_tensor(
                out=t[:, cols], in0=dw_bank[b][:], scalar=s1[:], in1=wc[:, cols], op0=ALU.subtract, op1=ALU.mult,
                accum_out=t_parts[:, b : b + 1],
            )
        t_sum = sb.tile([P, 1], F32, name="t_sum")
        nc.vector.tensor_scalar(
            out=t_sum[:], in0=t_parts[:, 0:1], scalar1=t_parts[:, 1:2], scalar2=1.0 / OUT_SCALE, op0=ALU.add, op1=ALU.mult
        )
        for c in range(n_ch):
            cols = slice(c * CH, (c + 1) * CH)
            y = sb.tile([P, CH], F32, name=f"y{c}", align_bytes=256)
            nc.vector.scalar_tensor_tensor(
                out=y[:], in0=u[:, cols], scalar=t_sum[:], in1=t[:, cols], op0=ALU.mult, op1=ALU.subtract
            )
            nc.sync.dma_start(out=out[:, cols], in_=y[:])
